import numpy as np
import ml_dtypes


def mxq(x, axis, fmt="e4m3"):
    dtype, down = {"e4m3": (ml_dtypes.float8_e4m3fn, 7), "e5m2": (ml_dtypes.float8_e5m2, 14)}[fmt]
    v = np.moveaxis(np.asarray(x, np.float32).astype(ml_dtypes.bfloat16).astype(np.float64), axis, -1)
    blocks = v.reshape(v.shape[:-1] + (-1, 32))
    amax = np.abs(blocks).max(-1, keepdims=True)
    byte = np.maximum(np.where(amax > 0, np.frexp(amax)[1] - 1 + 127, 0) - down, 1)
    scale = np.exp2(byte - 127.0)
    codes = (blocks / scale).astype(np.float32).astype(dtype).astype(np.float64)
    return np.moveaxis((codes * scale).reshape(v.shape), -1, axis)


WIDE = False


def mx_kscale(k):
    if not WIDE:
        return np.ones(k)
    levels = np.array([10, -10, 5, -5, 0])
    if k % 512:
        return np.exp2(np.random.permutation(np.resize(levels, k // 32))).repeat(32)
    a = np.empty((k // 512, 16))
    for p in range(k // 512):
        a[p, :8] = np.random.permutation(np.resize(levels, 8))
        for g in range(8):
            far = levels[np.abs(levels - a[p, g]) >= 10]
            a[p, g + 8] = far[np.random.randint(len(far))]
    return np.exp2(a.ravel()).repeat(32)


def f64(x):
    return np.asarray(x).astype(np.float64)


def striped(idx):
    return np.tile(idx.reshape(-1, 16).T, (8, 1)).astype(np.uint16)


def unstriped(offs):
    return offs[:16].T.reshape(-1).astype(np.int64)


def pack_weight(w):
    k, n = w.shape
    w = f64(np.asarray(w, np.float32).astype(ml_dtypes.bfloat16)).reshape(k // 32, 32, n)
    amax = np.abs(w).max(1)
    byte = np.clip(np.where(amax > 0, np.frexp(amax)[1] - 1 + 127 - 7, 1), 1, 254)
    scaled = (w * np.exp2(127.0 - byte)[:, None, :]).reshape(k, n).astype(np.float32)
    words = np.ascontiguousarray(scaled.reshape(k // 512, 128, 4, n).transpose(0, 1, 3, 2)).astype(ml_dtypes.float8_e4m3fn).view(np.uint8)
    return words, np.ascontiguousarray(byte.astype(np.uint8).reshape(k // 512, 16, n))


def unpack_weight(words, scales):
    g, p, n, _ = words.shape
    vals = np.ascontiguousarray(words).view(ml_dtypes.float8_e4m3fn).astype(np.float64) * np.repeat(np.exp2(scales.astype(np.float64) - 127.0), 8, axis=1)[..., None]
    return vals.transpose(0, 1, 3, 2).reshape(g * 512, n)


K, T, S, N = 512, 1024, 512, 256


def setup_inputs():
    n = np.random.standard_normal
    s = mx_kscale(K)[:, None]
    packed = pack_weight(n((K, T)) * s)
    return {
        "x_words": packed[0],
        "x_scales": packed[1],
        "w": (n((K, N)) / np.sqrt(K) / s).astype(np.float32),
        "b": (0.3 * n((N, 1))).astype(np.float32),
        "gate": np.tile(np.random.uniform(0.2, 1.0, S), (N, 1)).astype(np.float32),
        "offs": striped(np.random.permutation(T)[:S]),
    }


def reference(x_words, x_scales, w, b, gate, offs):
    idx = unstriped(offs)
    xq = unpack_weight(x_words, x_scales)[:, idx]
    y = mxq(f64(w), 0, "e4m3").T @ xq
    y = y + f64(b)
    out = np.zeros((N, T))
    out[:, idx] = f64(gate) * y
    return out

@@ -1,0 +1,113 @@
+from contextlib import ExitStack
+
+import concourse.mybir as mybir
+
+K, T, S, N = 512, 1024, 512, 256
+FLOPS = 2 * K * S * N
+BYTES = K * T + 16 * T + 4 * K * N + 4 * N + 4 * S + 2 * S + 4 * N * T
+
+F32 = mybir.dt.float32
+BF16 = mybir.dt.bfloat16
+I32 = mybir.dt.int32
+U32 = mybir.dt.uint32
+U16 = mybir.dt.uint16
+U8 = mybir.dt.uint8
+FP8X4 = mybir.dt.float8_e4m3fn_x4
+COPY = mybir.ActivationFunctionType.Copy
+IDENTITY = mybir.ActivationFunctionType.Identity
+MULT = mybir.AluOpType.mult
+
+P = 128
+PACK = 4
+HEAD = 128
+
+
+def tile_picked_depth_lin_bias_sub_p_kernel(tc, x_words, x_scales, w, b, gate, offs, out):
+    nc = tc.nc
+    with ExitStack() as ctx:
+        keep = ctx.enter_context(tc.tile_pool(name="keep", bufs=1))
+        psum = ctx.enter_context(tc.psum_pool(name="psum", bufs=1))
+
+        offsets = keep.tile([P, S // 16], U16, name="offsets")
+        scale_table = keep.tile([P, T], U8, name="scale_table", align_bytes=64)
+        word_table = keep.tile([P, T], I32, name="word_table", align_bytes=64)
+        w_raw = [keep.tile([P, PACK, P], F32, name="w_raw%d" % h, align_bytes=64) for h in range(2)]
+        gate_rows = keep.tile([P, S], F32, name="gate_rows", align_bytes=64)
+        bias = keep.tile([P, 2], F32, name="bias")
+        windows = [keep.tile([P, T], F32, name="window%d" % h, align_bytes=64) for h in range(2)]
+
+        nc.vector.memset(scale_table[:].bitcast(I32), 0)
+        w_rows = w.rearrange("(p j) n -> p j n", j=PACK)
+        nc.scalar.dma_start(out=w_raw[0][:], in_=w_rows[:, :, 0:P])
+        nc.sync.dma_start(offsets[:], offs)
+        for q in range(4):
+            nc.sync.dma_start(
+                out=scale_table[32 * q : 32 * q + 4, :].bitcast(I32),
+                in_=x_scales[0, 4 * q : 4 * q + 4, :].bitcast(I32),
+            )
+        nc.sync.dma_start(out=word_table[:], in_=x_words[0].rearrange("p c r -> p (c r)").bitcast(I32))
+        nc.sync.dma_start(out=gate_rows[:], in_=gate[0:P, :])
+        with nc.allow_non_contiguous_dma(reason="one bias value a partition"):
+            nc.gpsimd.dma_start(out=bias[:], in_=b.rearrange("(h p) o -> p (h o)", p=P))
+        nc.sync.dma_start(out=w_raw[1][:], in_=w_rows[:, :, P:N])
+        for h in range(2):
+            nc.vector.memset(windows[h][:], 0.0)
+
+        def cast(h):
+            grouped = keep.tile([P, P, PACK], BF16, name="grouped%d" % h, align_bytes=64)
+            nc.scalar.activation(
+                out=grouped[:].rearrange("p (c i) j -> p c j i", i=4),
+                in_=w_raw[h][:].rearrange("p j (c i) -> p c j i", i=4),
+                func=COPY,
+            )
+            return grouped
+
+        def quantise(h, grouped):
+            codes = keep.tile([P, P], U32, name="w_codes%d" % h, align_bytes=64)
+            scales = keep.tile([P, P], U8, name="w_scales%d" % h, align_bytes=64)
+            nc.vector.quantize_mx(
+                out=codes[:].bitcast(FP8X4), scales=scales[:], in_=grouped[:].rearrange("p c j -> p (c j)")
+            )
+            return codes, scales
+
+        picked_scales = keep.tile([P, S], U8, name="picked_scales", align_bytes=64)
+        picked_words = keep.tile([P, S], U32, name="picked_words", align_bytes=64)
+
+        def listed(lo, hi):
+            return offsets[:, lo // 16 : hi // 16]
+
+        def layer(h, weights, lo, hi, cuts):
+            codes, scales = weights
+            acc = psum.tile([P, hi - lo], F32, name="acc%d_%d" % (h, lo))
+            for a, z in cuts:
+                nc.tensor.matmul_mx(
+                    out=acc[:, a - lo : z - lo],
+                    lhsT=codes[:].bitcast(FP8X4),
+                    lhsT_scale=scales[:],
+                    rhs=picked_words[:, a:z].bitcast(FP8X4),
+                    rhs_scale=picked_scales[:, a:z],
+                    start=True,
+                    stop=True,
+                )
+            y = keep.tile([P, hi - lo], F32, name="y%d_%d" % (h, lo), align_bytes=64)
+            nc.scalar.activation(out=y[:], in_=acc[:], func=IDENTITY, bias=bias[:, h : h + 1])
+            return y
+
+        def put_back(h, y, lo, hi):
+            nc.vector.tensor_tensor(windows[h][:].indirect(listed(lo, hi)), y[:], gate_rows[:, lo:hi], MULT)
+
+        grouped0 = cast(0)
+        nc.vector.tensor_copy(picked_scales[:], scale_table[:].indirect(offsets[:]))
+        weights0 = quantise(0, grouped0)
+        for lo, hi in ((0, HEAD), (HEAD, S)):
+            nc.vector.tensor_copy(picked_words[:, lo:hi], word_table[:].bitcast(U32).indirect(listed(lo, hi)))
+        y_head = layer(0, weights0, 0, HEAD, [(0, HEAD)])
+        y_rest = layer(0, weights0, HEAD, S, [(HEAD, 256), (256, S)])
+        grouped1 = cast(1)
+        put_back(0, y_head, 0, HEAD)
+        weights1 = quantise(1, grouped1)
+        put_back(0, y_rest, HEAD, S)
+        nc.sync.dma_start(out=out[0:P, :], in_=windows[0][:])
+        y_second = layer(1, weights1, 0, S, [(0, S)])
+        put_back(1, y_second, 0, S)
+        nc.sync.dma_start(out=out[P:N, :], in_=windows[1][:])

@@ -31,33 +31,31 @@ def tile_picked_depth_lin_bias_sub_p_kernel(tc, x_words, x_scales, w, b, gate, o
         offsets = keep.tile([P, S // 16], U16, name="offsets")
         scale_table = keep.tile([P, T], U8, name="scale_table", align_bytes=64)
         word_table = keep.tile([P, T], I32, name="word_table", align_bytes=64)
-        w_raw = [keep.tile([P, PACK, P], F32, name="w_raw%d" % h, align_bytes=64) for h in range(2)]
+        w_raw = keep.tile([P, PACK, N], F32, name="w_raw", align_bytes=64)
         gate_rows = keep.tile([P, S], F32, name="gate_rows", align_bytes=64)
         bias = keep.tile([P, 2], F32, name="bias")
         windows = [keep.tile([P, T], F32, name="window%d" % h, align_bytes=64) for h in range(2)]
 
         nc.vector.memset(scale_table[:].bitcast(I32), 0)
-        w_rows = w.rearrange("(p j) n -> p j n", j=PACK)
-        nc.scalar.dma_start(out=w_raw[0][:], in_=w_rows[:, :, 0:P])
         nc.sync.dma_start(offsets[:], offs)
+        nc.sync.dma_start(out=w_raw[:], in_=w.rearrange("(p j) n -> p j n", j=PACK))
         for q in range(4):
             nc.sync.dma_start(
                 out=scale_table[32 * q : 32 * q + 4, :].bitcast(I32),
                 in_=x_scales[0, 4 * q : 4 * q + 4, :].bitcast(I32),
             )
         nc.sync.dma_start(out=word_table[:], in_=x_words[0].rearrange("p c r -> p (c r)").bitcast(I32))
-        nc.sync.dma_start(out=gate_rows[:], in_=gate[0:P, :])
         with nc.allow_non_contiguous_dma(reason="one bias value a partition"):
-            nc.gpsimd.dma_start(out=bias[:], in_=b.rearrange("(h p) o -> p (h o)", p=P))
-        nc.sync.dma_start(out=w_raw[1][:], in_=w_rows[:, :, P:N])
+            nc.sync.dma_start(out=bias[:], in_=b.rearrange("(h p) o -> p (h o)", p=P))
+        nc.sync.dma_start(out=gate_rows[:], in_=gate[0:P, :])
         for h in range(2):
-            nc.vector.memset(windows[h][:], 0.0)
+            nc.vector.memset(windows[h][:].bitcast(I32), 0)
 
         def cast(h):
             grouped = keep.tile([P, P, PACK], BF16, name="grouped%d" % h, align_bytes=64)
             nc.scalar.activation(
                 out=grouped[:].rearrange("p (c i) j -> p c j i", i=4),
-                in_=w_raw[h][:].rearrange("p j (c i) -> p c j i", i=4),
+                in_=w_raw[:, :, h * P : (h + 1) * P].rearrange("p j (c i) -> p c j i", i=4),
                 func=COPY,
             )
             return grouped
@@ -96,18 +94,17 @@ def tile_picked_depth_lin_bias_sub_p_kernel(tc, x_words, x_scales, w, b, gate, o
         def put_back(h, y, lo, hi):
             nc.vector.tensor_tensor(windows[h][:].indirect(listed(lo, hi)), y[:], gate_rows[:, lo:hi], MULT)
 
-        grouped0 = cast(0)
+        grouped = [cast(h) for h in range(2)]
         nc.vector.tensor_copy(picked_scales[:], scale_table[:].indirect(offsets[:]))
-        weights0 = quantise(0, grouped0)
-        for lo, hi in ((0, HEAD), (HEAD, S)):
-            nc.vector.tensor_copy(picked_words[:, lo:hi], word_table[:].bitcast(U32).indirect(listed(lo, hi)))
+        weights0 = quantise(0, grouped[0])
+        nc.vector.tensor_copy(picked_words[:, 0:HEAD], word_table[:].bitcast(U32).indirect(listed(0, HEAD)))
+        weights1 = quantise(1, grouped[1])
+        nc.vector.tensor_copy(picked_words[:, HEAD:S], word_table[:].bitcast(U32).indirect(listed(HEAD, S)))
         y_head = layer(0, weights0, 0, HEAD, [(0, HEAD)])
         y_rest = layer(0, weights0, HEAD, S, [(HEAD, 256), (256, S)])
-        grouped1 = cast(1)
+        y_second = layer(1, weights1, 0, S, [(0, S)])
         put_back(0, y_head, 0, HEAD)
-        weights1 = quantise(1, grouped1)
         put_back(0, y_rest, HEAD, S)
         nc.sync.dma_start(out=out[0:P, :], in_=windows[0][:])
-        y_second = layer(1, weights1, 0, S, [(0, S)])
         put_back(1, y_second, 0, S)
         nc.sync.dma_start(out=out[P:N, :], in_=windows[1][:])

@@ -36,23 +36,23 @@ def tile_picked_depth_lin_bias_sub_p_kernel(tc, x_words, x_scales, w, b, gate, o
         bias = keep.tile([P, 2], F32, name="bias")
         windows = [keep.tile([P, T], F32, name="window%d" % h, align_bytes=64) for h in range(2)]
 
-        nc.vector.memset(scale_table[:].bitcast(I32), 0)
-        nc.sync.dma_start(offsets[:], offs)
-        nc.sync.dma_start(out=w_raw[:], in_=w.rearrange("(p j) n -> p j n", j=PACK))
+        nc.gpsimd.memset(scale_table[:].bitcast(I32), 0)
         for q in range(4):
-            nc.sync.dma_start(
+            nc.scalar.dma_start(
                 out=scale_table[32 * q : 32 * q + 4, :].bitcast(I32),
                 in_=x_scales[0, 4 * q : 4 * q + 4, :].bitcast(I32),
             )
+        nc.sync.dma_start(offsets[:], offs)
+        nc.sync.dma_start(out=w_raw[:], in_=w.rearrange("(p j) n -> p j n", j=PACK))
         nc.sync.dma_start(out=word_table[:], in_=x_words[0].rearrange("p c r -> p (c r)").bitcast(I32))
-        with nc.allow_non_contiguous_dma(reason="one bias value a partition"):
-            nc.sync.dma_start(out=bias[:], in_=b.rearrange("(h p) o -> p (h o)", p=P))
         nc.sync.dma_start(out=gate_rows[:], in_=gate[0:P, :])
+        with nc.allow_non_contiguous_dma(reason="one bias value a partition"):
+            nc.gpsimd.dma_start(out=bias[:], in_=b.rearrange("(h p) o -> p (h o)", p=P))
         for h in range(2):
             nc.vector.memset(windows[h][:].bitcast(I32), 0)
 
         def cast(h):
-            grouped = keep.tile([P, P, PACK], BF16, name="grouped%d" % h, align_bytes=64)
+            grouped = keep.tile([P, P, PACK], BF16, name="grouped%d" % h, tag="stage%d" % h, align_bytes=64)
             nc.scalar.activation(
                 out=grouped[:].rearrange("p (c i) j -> p c j i", i=4),
                 in_=w_raw[:, :, h * P : (h + 1) * P].rearrange("p j (c i) -> p c j i", i=4),
@@ -69,7 +69,6 @@ def tile_picked_depth_lin_bias_sub_p_kernel(tc, x_words, x_scales, w, b, gate, o
             return codes, scales
 
         picked_scales = keep.tile([P, S], U8, name="picked_scales", align_bytes=64)
-        picked_words = keep.tile([P, S], U32, name="picked_words", align_bytes=64)
 
         def listed(lo, hi):
             return offsets[:, lo // 16 : hi // 16]
@@ -94,17 +93,15 @@ def tile_picked_depth_lin_bias_sub_p_kernel(tc, x_words, x_scales, w, b, gate, o
         def put_back(h, y, lo, hi):
             nc.vector.tensor_tensor(windows[h][:].indirect(listed(lo, hi)), y[:], gate_rows[:, lo:hi], MULT)
 
-        grouped = [cast(h) for h in range(2)]
         nc.vector.tensor_copy(picked_scales[:], scale_table[:].indirect(offsets[:]))
-        weights0 = quantise(0, grouped[0])
-        nc.vector.tensor_copy(picked_words[:, 0:HEAD], word_table[:].bitcast(U32).indirect(listed(0, HEAD)))
-        weights1 = quantise(1, grouped[1])
-        nc.vector.tensor_copy(picked_words[:, HEAD:S], word_table[:].bitcast(U32).indirect(listed(HEAD, S)))
-        y_head = layer(0, weights0, 0, HEAD, [(0, HEAD)])
-        y_rest = layer(0, weights0, HEAD, S, [(HEAD, 256), (256, S)])
-        y_second = layer(1, weights1, 0, S, [(0, S)])
-        put_back(0, y_head, 0, HEAD)
-        put_back(0, y_rest, HEAD, S)
-        nc.sync.dma_start(out=out[0:P, :], in_=windows[0][:])
-        put_back(1, y_second, 0, S)
-        nc.sync.dma_start(out=out[P:N, :], in_=windows[1][:])
+        grouped = [cast(h) for h in range(2)]
+        weights = [quantise(h, grouped[h]) for h in range(2)]
+        picked_words = keep.tile([P, S], U32, name="picked_words", tag="stage0", align_bytes=64)
+        pieces = ((0, HEAD, [(0, HEAD)]), (HEAD, S, [(HEAD, 256), (256, S)]))
+        for lo, hi, cuts in pieces:
+            nc.vector.tensor_copy(picked_words[:, lo:hi], word_table[:].bitcast(U32).indirect(listed(lo, hi)))
+        for lo, hi, cuts in pieces:
+            for h in range(2):
+                put_back(h, layer(h, weights[h], lo, hi, cuts), lo, hi)
+                if hi == S:
+                    nc.sync.dma_start(out=out[h * P : (h + 1) * P, :], in_=windows[h][:])

@@ -36,23 +36,23 @@ def tile_picked_depth_lin_bias_sub_p_kernel(tc, x_words, x_scales, w, b, gate, o
         bias = keep.tile([P, 2], F32, name="bias")
         windows = [keep.tile([P, T], F32, name="window%d" % h, align_bytes=64) for h in range(2)]
 
-        nc.gpsimd.memset(scale_table[:].bitcast(I32), 0)
+        nc.vector.memset(scale_table[:].bitcast(I32), 0)
+        nc.sync.dma_start(offsets[:], offs)
+        nc.sync.dma_start(out=w_raw[:], in_=w.rearrange("(p j) n -> p j n", j=PACK))
         for q in range(4):
-            nc.scalar.dma_start(
+            nc.sync.dma_start(
                 out=scale_table[32 * q : 32 * q + 4, :].bitcast(I32),
                 in_=x_scales[0, 4 * q : 4 * q + 4, :].bitcast(I32),
             )
-        nc.sync.dma_start(offsets[:], offs)
-        nc.sync.dma_start(out=w_raw[:], in_=w.rearrange("(p j) n -> p j n", j=PACK))
         nc.sync.dma_start(out=word_table[:], in_=x_words[0].rearrange("p c r -> p (c r)").bitcast(I32))
-        nc.sync.dma_start(out=gate_rows[:], in_=gate[0:P, :])
         with nc.allow_non_contiguous_dma(reason="one bias value a partition"):
-            nc.gpsimd.dma_start(out=bias[:], in_=b.rearrange("(h p) o -> p (h o)", p=P))
+            nc.sync.dma_start(out=bias[:], in_=b.rearrange("(h p) o -> p (h o)", p=P))
+        nc.sync.dma_start(out=gate_rows[:], in_=gate[0:P, :])
         for h in range(2):
             nc.vector.memset(windows[h][:].bitcast(I32), 0)
 
         def cast(h):
-            grouped = keep.tile([P, P, PACK], BF16, name="grouped%d" % h, tag="stage%d" % h, align_bytes=64)
+            grouped = keep.tile([P, P, PACK], BF16, name="grouped%d" % h, align_bytes=64)
             nc.scalar.activation(
                 out=grouped[:].rearrange("p (c i) j -> p c j i", i=4),
                 in_=w_raw[:, :, h * P : (h + 1) * P].rearrange("p j (c i) -> p c j i", i=4),
@@ -96,7 +96,7 @@ def tile_picked_depth_lin_bias_sub_p_kernel(tc, x_words, x_scales, w, b, gate, o
         nc.vector.tensor_copy(picked_scales[:], scale_table[:].indirect(offsets[:]))
         grouped = [cast(h) for h in range(2)]
         weights = [quantise(h, grouped[h]) for h in range(2)]
-        picked_words = keep.tile([P, S], U32, name="picked_words", tag="stage0", align_bytes=64)
+        picked_words = keep.tile([P, S], U32, name="picked_words", align_bytes=64)
         pieces = ((0, HEAD, [(0, HEAD)]), (HEAD, S, [(HEAD, 256), (256, S)]))
         for lo, hi, cuts in pieces:
             nc.vector.tensor_copy(picked_words[:, lo:hi], word_table[:].bitcast(U32).indirect(listed(lo, hi)))

from contextlib import ExitStack

import concourse.mybir as mybir

K, T, S, N = 512, 1024, 512, 256
FLOPS = 2 * K * S * N
BYTES = K * T + 16 * T + 4 * K * N + 4 * N + 4 * S + 2 * S + 4 * N * T

F32 = mybir.dt.float32
BF16 = mybir.dt.bfloat16
I32 = mybir.dt.int32
U32 = mybir.dt.uint32
U16 = mybir.dt.uint16
U8 = mybir.dt.uint8
FP8X4 = mybir.dt.float8_e4m3fn_x4
COPY = mybir.ActivationFunctionType.Copy
IDENTITY = mybir.ActivationFunctionType.Identity
MULT = mybir.AluOpType.mult

P = 128
PACK = 4
HEAD = 128


def tile_picked_depth_lin_bias_sub_p_kernel(tc, x_words, x_scales, w, b, gate, offs, out):
    nc = tc.nc
    with ExitStack() as ctx:
        keep = ctx.enter_context(tc.tile_pool(name="keep", bufs=1))
        psum = ctx.enter_context(tc.psum_pool(name="psum", bufs=1))

        offsets = keep.tile([P, S // 16], U16, name="offsets")
        scale_table = keep.tile([P, T], U8, name="scale_table", align_bytes=64)
        word_table = keep.tile([P, T], I32, name="word_table", align_bytes=64)
        w_raw = keep.tile([P, PACK, N], F32, name="w_raw", align_bytes=64)
        gate_rows = keep.tile([P, S], F32, name="gate_rows", align_bytes=64)
        bias = keep.tile([P, 2], F32, name="bias")
        windows = [keep.tile([P, T], F32, name="window%d" % h, align_bytes=64) for h in range(2)]

        nc.vector.memset(scale_table[:].bitcast(I32), 0)
        nc.sync.dma_start(offsets[:], offs)
        nc.sync.dma_start(out=w_raw[:], in_=w.rearrange("(p j) n -> p j n", j=PACK))
        for q in range(4):
            nc.sync.dma_start(
                out=scale_table[32 * q : 32 * q + 4, :].bitcast(I32),
                in_=x_scales[0, 4 * q : 4 * q + 4, :].bitcast(I32),
            )
        nc.sync.dma_start(out=word_table[:], in_=x_words[0].rearrange("p c r -> p (c r)").bitcast(I32))
        with nc.allow_non_contiguous_dma(reason="one bias value a partition"):
            nc.sync.dma_start(out=bias[:], in_=b.rearrange("(h p) o -> p (h o)", p=P))
        nc.sync.dma_start(out=gate_rows[:], in_=gate[0:P, :])
        for h in range(2):
            nc.vector.memset(windows[h][:].bitcast(I32), 0)

        def cast(h):
            grouped = keep.tile([P, P, PACK], BF16, name="grouped%d" % h, align_bytes=64)
            nc.scalar.activation(
                out=grouped[:].rearrange("p (c i) j -> p c j i", i=4),
                in_=w_raw[:, :, h * P : (h + 1) * P].rearrange("p j (c i) -> p c j i", i=4),
                func=COPY,
            )
            return grouped

        def quantise(h, grouped):
            codes = keep.tile([P, P], U32, name="w_codes%d" % h, align_bytes=64)
            scales = keep.tile([P, P], U8, name="w_scales%d" % h, align_bytes=64)
            nc.vector.quantize_mx(
                out=codes[:].bitcast(FP8X4), scales=scales[:], in_=grouped[:].rearrange("p c j -> p (c j)")
            )
            return codes, scales

        picked_scales = keep.tile([P, S], U8, name="picked_scales", align_bytes=64)

        def listed(lo, hi):
            return offsets[:, lo // 16 : hi // 16]

        def layer(h, weights, lo, hi, cuts):
            codes, scales = weights
            acc = psum.tile([P, hi - lo], F32, name="acc%d_%d" % (h, lo))
            for a, z in cuts:
                nc.tensor.matmul_mx(
                    out=acc[:, a - lo : z - lo],
                    lhsT=codes[:].bitcast(FP8X4),
                    lhsT_scale=scales[:],
                    rhs=picked_words[:, a:z].bitcast(FP8X4),
                    rhs_scale=picked_scales[:, a:z],
                    start=True,
                    stop=True,
                )
            y = keep.tile([P, hi - lo], F32, name="y%d_%d" % (h, lo), align_bytes=64)
            nc.scalar.activation(out=y[:], in_=acc[:], func=IDENTITY, bias=bias[:, h : h + 1])
            return y

        def put_back(h, y, lo, hi):
            nc.vector.tensor_tensor(windows[h][:].indirect(listed(lo, hi)), y[:], gate_rows[:, lo:hi], MULT)

        nc.vector.tensor_copy(picked_scales[:], scale_table[:].indirect(offsets[:]))
        grouped = [cast(h) for h in range(2)]
        weights = [quantise(h, grouped[h]) for h in range(2)]
        picked_words = keep.tile([P, S], U32, name="picked_words", align_bytes=64)
        pieces = ((0, HEAD, [(0, HEAD)]), (HEAD, S, [(HEAD, 256), (256, S)]))
        for lo, hi, cuts in pieces:
            nc.vector.tensor_copy(picked_words[:, lo:hi], word_table[:].bitcast(U32).indirect(listed(lo, hi)))
        for lo, hi, cuts in pieces:
            for h in range(2):
                put_back(h, layer(h, weights[h], lo, hi, cuts), lo, hi)
                if hi == S:
                    nc.sync.dma_start(out=out[h * P : (h + 1) * P, :], in_=windows[h][:])
